import numpy as np
import ml_dtypes


def mxq(x, axis, fmt="e4m3"):
    dtype, down = {"e4m3": (ml_dtypes.float8_e4m3fn, 7), "e5m2": (ml_dtypes.float8_e5m2, 14)}[fmt]
    v = np.moveaxis(np.asarray(x, np.float32).astype(ml_dtypes.bfloat16).astype(np.float64), axis, -1)
    blocks = v.reshape(v.shape[:-1] + (-1, 32))
    amax = np.abs(blocks).max(-1, keepdims=True)
    byte = np.maximum(np.where(amax > 0, np.frexp(amax)[1] - 1 + 127, 0) - down, 1)
    scale = np.exp2(byte - 127.0)
    codes = (blocks / scale).astype(np.float32).astype(dtype).astype(np.float64)
    return np.moveaxis((codes * scale).reshape(v.shape), -1, axis)


WIDE = False


def mx_kscale(k):
    if not WIDE:
        return np.ones(k)
    levels = np.array([10, -10, 5, -5, 0])
    if k % 512:
        return np.exp2(np.random.permutation(np.resize(levels, k // 32))).repeat(32)
    a = np.empty((k // 512, 16))
    for p in range(k // 512):
        a[p, :8] = np.random.permutation(np.resize(levels, 8))
        for g in range(8):
            far = levels[np.abs(levels - a[p, g]) >= 10]
            a[p, g + 8] = far[np.random.randint(len(far))]
    return np.exp2(a.ravel()).repeat(32)


def f64(x):
    return np.asarray(x).astype(np.float64)


def striped(idx):
    return np.tile(np.asarray(idx).reshape(-1, 16).T, (8, 1)).astype(np.uint16)


def unstriped(offs):
    return offs[:16].T.reshape(-1).astype(np.int64)


E2M1 = np.array([0.0, 0.5, 1.0, 1.5, 2.0, 3.0, 4.0, 6.0, -0.0, -0.5, -1.0, -1.5, -2.0, -3.0, -4.0, -6.0])


def pack_weight(w, fmt):
    k, n = w.shape
    w = f64(np.asarray(w, np.float32).astype(ml_dtypes.bfloat16)).reshape(k // 32, 32, n)
    amax = np.abs(w).max(1)
    if fmt == "e4m3":
        byte = np.frexp(amax)[1] - 1 + 127 - 7
    else:
        mant, ex = np.frexp(amax / 6.0)
        byte = np.where(mant > 0.5, ex, ex - 1) + 127
    byte = np.clip(np.where(amax > 0, byte, 1), 1, 254)
    scaled = (w * np.exp2(127.0 - byte)[:, None, :]).reshape(k, n).astype(np.float32)
    by_word = np.ascontiguousarray(scaled.reshape(k // 512, 128, 4, n).transpose(0, 1, 3, 2))
    if fmt == "e4m3":
        words = by_word.astype(ml_dtypes.float8_e4m3fn).view(np.uint8)
    else:
        c = by_word.astype(ml_dtypes.float4_e2m1fn).view(np.uint8) & 0xF
        words = (c[..., 0::2] | (c[..., 1::2] << 4)).reshape(k // 512, 128, 2 * n)
    return np.ascontiguousarray(words), np.ascontiguousarray(byte.astype(np.uint8).reshape(k // 512, 16, n))


def unpack_weight(words, scales, fmt):
    g, _, n = scales.shape
    words = np.ascontiguousarray(words).reshape(g, 128, n, -1)
    if fmt == "e4m3":
        vals = words.view(ml_dtypes.float8_e4m3fn).astype(np.float64)
    else:
        nib = np.empty((g, 128, n, 4), np.uint8)
        nib[..., 0::2] = words & 0xF
        nib[..., 1::2] = words >> 4
        vals = E2M1[nib]
    vals = vals * np.repeat(np.exp2(scales.astype(np.float64) - 127.0), 8, axis=1)[..., None]
    return vals.transpose(0, 1, 3, 2).reshape(g * 512, n)


B, N, T, D, NQ = 1, 1024, 4096, 1024, 128
SEG = 32


def setup_inputs():
    n = np.random.standard_normal
    pages = np.random.permutation(T // 32)[:B * N // 32]
    idx = (pages[:, None] * 32 + np.arange(32)[None, :]).reshape(-1)
    s = mx_kscale(D)[:, None]
    kp = pack_weight(n((D, T)) / s, "e2m1")
    return {
        "qT": (n((B, D, NQ)) * s * (1.00 / np.sqrt(D))).astype(np.float32),
        "k_words": np.ascontiguousarray(kp[0].reshape(1, 2, 128, T, 2).transpose(0, 2, 3, 1, 4)).reshape(1, 128, T, 4),
        "k_scales": kp[1],
        "offs": striped(idx),
    }


def reference(qT, k_words, k_scales, offs):
    idx = unstriped(offs)
    pick = lambda x, which: x[:, which].reshape(x.shape[0], B, -1).transpose(1, 0, 2)
    k = unpack_weight(k_words.reshape(1, 128, T, 2, 2).transpose(0, 3, 1, 2, 4).reshape(2, 128, 2 * T), k_scales, "e2m1")
    kg = pick(k, idx)
    qq = mxq(f64(qT), 1, "e4m3")
    a = qq.transpose(0, 2, 1) @ kg
    m = np.max(a, axis=-1, keepdims=True)
    e = np.exp(a - m)
    l = np.sum(e, axis=-1, keepdims=True)
    y = e.reshape(B, NQ, N // SEG, SEG).max(-1) / l
    return y

@@ -1,0 +1,134 @@
+from contextlib import ExitStack
+
+import concourse.mybir as mybir
+
+T, D, NQ, N, SEG = 4096, 1024, 128, 1024, 32
+FLOPS = 2 * NQ * D * N
+
+F32 = mybir.dt.float32
+BF16 = mybir.dt.bfloat16
+I32 = mybir.dt.int32
+U32 = mybir.dt.uint32
+U16 = mybir.dt.uint16
+U8 = mybir.dt.uint8
+FP8X4 = mybir.dt.float8_e4m3fn_x4
+FP4X4 = mybir.dt.float4_e2m1fn_x4
+ACT = mybir.ActivationFunctionType
+ALU = mybir.AluOpType
+AX = mybir.AxisListType
+
+P = 128
+PACK = 4
+K_PASS = P * PACK
+PASSES = D // K_PASS
+CHUNK = 512
+CHUNKS = N // CHUNK
+PAGES = N // SEG
+CHUNK_PAGES = CHUNK // SEG
+
+
+def tile_attend_page_peak_kernel(tc, qT, k_words, k_scales, offs, out):
+    nc = tc.nc
+    with ExitStack() as ctx:
+        sb = ctx.enter_context(tc.tile_pool(name="sb", bufs=1))
+        ps = ctx.enter_context(tc.psum_pool(name="ps", bufs=1))
+
+        offsets = sb.tile([P, N // 16], U16, name="offsets")
+        word_pool = sb.tile([P, T], U32, name="word_pool", align_bytes=64)
+        byte_pool = sb.tile([P, T], U8, name="byte_pool", align_bytes=64)
+        byte_listed = sb.tile([P, N], U8, name="byte_listed", align_bytes=64)
+        k_planes = sb.tile([P, PASSES, N], U8, name="k_planes", align_bytes=64)
+
+        nc.vector.memset(byte_pool[:].bitcast(I32), 0)
+        nc.vector.memset(k_planes[:].rearrange("p o n -> p (o n)").bitcast(I32), 0)
+
+        nc.sync.dma_start(offsets[:], offs)
+        nc.sync.dma_start(word_pool[:].bitcast(I32), k_words[0].rearrange("p t b -> p (t b)").bitcast(I32))
+        nc.scalar.dma_start(byte_pool[0:P:4, :].bitcast(I32), k_scales.rearrange("o f t -> f o t").bitcast(I32))
+        q_raw = [sb.tile([P, PACK, NQ], F32, name=f"q_raw{o}") for o in range(PASSES)]
+        for o in range(PASSES):
+            nc.sync.dma_start(q_raw[o][:], qT[0, o * K_PASS : (o + 1) * K_PASS, :].rearrange("(p j) q -> p j q", j=PACK))
+
+        nc.vector.tensor_copy(byte_listed[:], byte_pool[:].indirect(offsets[:]))
+        for quad in range(4):
+            nc.sync.dma_start(
+                k_planes[32 * quad : 32 * quad + 4, :, :].rearrange("p o n -> p (o n)").bitcast(I32),
+                byte_listed[32 * quad : 32 * quad + 32 : 4, :].bitcast(I32),
+            )
+
+        q_bf = [sb.tile([P, NQ, PACK], BF16, name=f"q_bf{o}", align_bytes=64) for o in range(PASSES)]
+        q_codes = [sb.tile([P, NQ], U32, name=f"q_codes{o}", align_bytes=64) for o in range(PASSES)]
+        q_planes = [sb.tile([P, NQ], U8, name=f"q_planes{o}", align_bytes=64) for o in range(PASSES)]
+        listed = [sb.tile([P, CHUNK], U32, name=f"listed{c}", align_bytes=64) for c in range(CHUNKS)]
+        k_codes = [[sb.tile([P, CHUNK], U16, name=f"k_codes{c}_{o}", align_bytes=64) for o in range(PASSES)] for c in range(CHUNKS)]
+        scores = [ps.tile([P, CHUNK], F32, name=f"scores{c}") for c in range(CHUNKS)]
+
+        def cast(o):
+            nc.scalar.activation(q_bf[o][:], q_raw[o][:].rearrange("p j q -> p q j"), ACT.Copy)
+
+        def quantise(o):
+            nc.vector.quantize_mx(out=q_codes[o][:].bitcast(FP8X4), scales=q_planes[o][:], in_=q_bf[o][:].rearrange("p q j -> p (q j)"))
+
+        def gather(c):
+            cols = CHUNK // 16
+            nc.vector.tensor_copy(listed[c][:], word_pool[:].indirect(offsets[:, c * cols : (c + 1) * cols]))
+
+        def part(c, o):
+            halves = listed[c][:].bitcast(U16).rearrange("p (n o) -> p o n", o=PASSES)
+            nc.vector.tensor_copy(k_codes[c][o][:], halves[:, o, :])
+
+        def multiply(c, o):
+            nc.tensor.matmul_mx(
+                out=scores[c][:],
+                lhsT=q_codes[o][:].bitcast(FP8X4),
+                lhsT_scale=q_planes[o][:],
+                rhs=k_codes[c][o][:].bitcast(FP4X4),
+                rhs_scale=k_planes[:, o, c * CHUNK : (c + 1) * CHUNK],
+                start=(o == 0),
+                stop=(o == PASSES - 1),
+            )
+
+        neg_peak = sb.tile([P, PAGES + 1], F32, name="neg_peak")
+        neg_max = sb.tile([P, 1], F32, name="neg_max")
+        sums = sb.tile([P, CHUNKS], F32, name="sums")
+        weights = [sb.tile([P, CHUNK], F32, name=f"weights{c}") for c in range(CHUNKS)]
+        peak = sb.tile([P, PAGES + 1], F32, name="peak")
+        total = sb.tile([P, 1], F32, name="total")
+        inverse = sb.tile([P, 1], F32, name="inverse")
+        result = sb.tile([P, PAGES], F32, name="result")
+
+        def page_peaks(c):
+            nc.vector.tensor_reduce(
+                neg_peak[:, c * CHUNK_PAGES : (c + 1) * CHUNK_PAGES],
+                scores[c][:].rearrange("p (j s) -> p j s", s=SEG),
+                AX.X,
+                ALU.max,
+                negate=True,
+            )
+
+        cast(0)
+        cast(1)
+        gather(0)
+        part(0, 0)
+        gather(1)
+        quantise(0)
+        part(1, 0)
+        multiply(0, 0)
+        part(0, 1)
+        multiply(1, 0)
+        quantise(1)
+        part(1, 1)
+        multiply(0, 1)
+        multiply(1, 1)
+
+        page_peaks(0)
+        nc.vector.tensor_reduce(neg_peak[:, PAGES : PAGES + 1], neg_peak[:, 0:CHUNK_PAGES], AX.X, ALU.min)
+        nc.scalar.activation(weights[0][:], scores[0][:], ACT.Exp, bias=neg_peak[:, PAGES : PAGES + 1], accum_out=sums[:, 0:1])
+        page_peaks(1)
+        nc.vector.tensor_reduce(neg_max[:], neg_peak[:, 0:PAGES], AX.X, ALU.min)
+        nc.scalar.activation(peak[:], neg_peak[:], ACT.Exp, bias=neg_max[:], scale=-1.0)
+        nc.scalar.activation(weights[1][:], scores[1][:], ACT.Exp, bias=neg_max[:], accum_out=sums[:, 1:2])
+        nc.vector.tensor_scalar(total[:], sums[:, 0:1], peak[:, PAGES : PAGES + 1], sums[:, 1:2], ALU.mult, ALU.add)
+        nc.vector.reciprocal(inverse[:], total[:])
+        nc.vector.tensor_scalar(result[:], peak[:, 0:PAGES], inverse[:], None, ALU.mult)
+        nc.sync.dma_start(out[0], result[:])

@@ -39,21 +39,22 @@ def tile_attend_page_peak_kernel(tc, qT, k_words, k_scales, offs, out):
         byte_listed = sb.tile([P, N], U8, name="byte_listed", align_bytes=64)
         k_planes = sb.tile([P, PASSES, N], U8, name="k_planes", align_bytes=64)
 
-        nc.vector.memset(byte_pool[:].bitcast(I32), 0)
+        nc.vector.memset(byte_pool[32:64, :].bitcast(I32), 0)
+        nc.vector.memset(byte_pool[64:P, :].bitcast(I32), 0)
         nc.vector.memset(k_planes[:].rearrange("p o n -> p (o n)").bitcast(I32), 0)
 
         nc.sync.dma_start(offsets[:], offs)
+        nc.sync.dma_start(byte_pool[0:32, :].bitcast(I32), k_scales.rearrange("o f t -> f o t").bitcast(I32))
         nc.sync.dma_start(word_pool[:].bitcast(I32), k_words[0].rearrange("p t b -> p (t b)").bitcast(I32))
-        nc.scalar.dma_start(byte_pool[0:P:4, :].bitcast(I32), k_scales.rearrange("o f t -> f o t").bitcast(I32))
         q_raw = [sb.tile([P, PACK, NQ], F32, name=f"q_raw{o}") for o in range(PASSES)]
         for o in range(PASSES):
             nc.sync.dma_start(q_raw[o][:], qT[0, o * K_PASS : (o + 1) * K_PASS, :].rearrange("(p j) q -> p j q", j=PACK))
 
         nc.vector.tensor_copy(byte_listed[:], byte_pool[:].indirect(offsets[:]))
         for quad in range(4):
-            nc.sync.dma_start(
+            nc.scalar.dma_start(
                 k_planes[32 * quad : 32 * quad + 4, :, :].rearrange("p o n -> p (o n)").bitcast(I32),
-                byte_listed[32 * quad : 32 * quad + 32 : 4, :].bitcast(I32),
+                byte_listed[8 * quad : 8 * quad + 8, :].bitcast(I32),
             )
 
         q_bf = [sb.tile([P, NQ, PACK], BF16, name=f"q_bf{o}", align_bytes=64) for o in range(PASSES)]
@@ -112,13 +113,13 @@ def tile_attend_page_peak_kernel(tc, qT, k_words, k_scales, offs, out):
         part(0, 0)
         gather(1)
         quantise(0)
-        part(1, 0)
-        multiply(0, 0)
         part(0, 1)
-        multiply(1, 0)
         quantise(1)
-        part(1, 1)
+        multiply(0, 0)
         multiply(0, 1)
+        part(1, 0)
+        part(1, 1)
+        multiply(1, 0)
         multiply(1, 1)
 
         page_peaks(0)

@@ -1,6 +1,7 @@
 from contextlib import ExitStack
 
 import concourse.mybir as mybir
+from concourse.masks import make_identity
 
 T, D, NQ, N, SEG = 4096, 1024, 128, 1024, 32
 FLOPS = 2 * NQ * D * N
@@ -21,6 +22,7 @@ P = 128
 PACK = 4
 K_PASS = P * PACK
 PASSES = D // K_PASS
+WARM_UP = 92
 CHUNK = 512
 CHUNKS = N // CHUNK
 PAGES = N // SEG
@@ -106,6 +108,12 @@ def tile_attend_page_peak_kernel(tc, qT, k_words, k_scales, offs, out):
                 ALU.max,
                 negate=True,
             )
+
+        identity = sb.tile([P, P], BF16, name="identity")
+        make_identity(nc, identity[:])
+        idle = [ps.tile([P, 8, P], BF16, name=f"idle{b}") for b in range(6)]
+        for i in range(WARM_UP):
+            nc.tensor.transpose(idle[i % 6][:, (i // 6) % 8, :], identity[:], identity[:])
 
         cast(0)
         cast(1)

@@ -23,6 +23,7 @@ PACK = 4
 K_PASS = P * PACK
 PASSES = D // K_PASS
 WARM_UP = 92
+BRIDGE = 10
 CHUNK = 512
 CHUNKS = N // CHUNK
 PAGES = N // SEG
@@ -53,8 +54,8 @@ def tile_attend_page_peak_kernel(tc, qT, k_words, k_scales, offs, out):
             nc.sync.dma_start(q_raw[o][:], qT[0, o * K_PASS : (o + 1) * K_PASS, :].rearrange("(p j) q -> p j q", j=PACK))
 
         nc.vector.tensor_copy(byte_listed[:], byte_pool[:].indirect(offsets[:]))
-        for quad in range(4):
-            nc.scalar.dma_start(
+        for quad in (0, 2, 1, 3):
+            nc.sync.dma_start(
                 k_planes[32 * quad : 32 * quad + 4, :, :].rearrange("p o n -> p (o n)").bitcast(I32),
                 byte_listed[8 * quad : 8 * quad + 8, :].bitcast(I32),
             )
@@ -117,6 +118,9 @@ def tile_attend_page_peak_kernel(tc, qT, k_words, k_scales, offs, out):
 
         cast(0)
         cast(1)
+        q_cols = q_bf[0][:].rearrange("p q j -> p (q j)")
+        for i in range(WARM_UP, WARM_UP + BRIDGE):
+            nc.tensor.transpose(idle[i % 6][:, (i // 6) % 8, :], q_cols[:, (i % 4) * P : (i % 4 + 1) * P], identity[:])
         gather(0)
         part(0, 0)
         gather(1)

@@ -1,7 +1,6 @@
 from contextlib import ExitStack
 
 import concourse.mybir as mybir
-from concourse.masks import make_identity
 
 T, D, NQ, N, SEG = 4096, 1024, 128, 1024, 32
 FLOPS = 2 * NQ * D * N
@@ -22,12 +21,13 @@ P = 128
 PACK = 4
 K_PASS = P * PACK
 PASSES = D // K_PASS
-WARM_UP = 92
-BRIDGE = 10
-CHUNK = 512
-CHUNKS = N // CHUNK
+GATHER = 512
+GROUP = 128
+WIDTHS = (256, 256, 256, 128, 128)
+STARTS = tuple(sum(WIDTHS[:i]) for i in range(len(WIDTHS)))
+PIECES = len(WIDTHS)
+LAST = PIECES - 1
 PAGES = N // SEG
-CHUNK_PAGES = CHUNK // SEG
 
 
 def tile_attend_page_peak_kernel(tc, qT, k_words, k_scales, offs, out):
@@ -49,7 +49,7 @@ def tile_attend_page_peak_kernel(tc, qT, k_words, k_scales, offs, out):
         nc.sync.dma_start(offsets[:], offs)
         nc.sync.dma_start(byte_pool[0:32, :].bitcast(I32), k_scales.rearrange("o f t -> f o t").bitcast(I32))
         nc.sync.dma_start(word_pool[:].bitcast(I32), k_words[0].rearrange("p t b -> p (t b)").bitcast(I32))
-        q_raw = [sb.tile([P, PACK, NQ], F32, name=f"q_raw{o}") for o in range(PASSES)]
+        q_raw = [sb.tile([P, PACK, NQ], F32, name=f"q_raw{o}", tag=f"after_cast{o}", align_bytes=64) for o in range(PASSES)]
         for o in range(PASSES):
             nc.sync.dma_start(q_raw[o][:], qT[0, o * K_PASS : (o + 1) * K_PASS, :].rearrange("(p j) q -> p j q", j=PACK))
 
@@ -63,85 +63,85 @@ def tile_attend_page_peak_kernel(tc, qT, k_words, k_scales, offs, out):
         q_bf = [sb.tile([P, NQ, PACK], BF16, name=f"q_bf{o}", align_bytes=64) for o in range(PASSES)]
         q_codes = [sb.tile([P, NQ], U32, name=f"q_codes{o}", align_bytes=64) for o in range(PASSES)]
         q_planes = [sb.tile([P, NQ], U8, name=f"q_planes{o}", align_bytes=64) for o in range(PASSES)]
-        listed = [sb.tile([P, CHUNK], U32, name=f"listed{c}", align_bytes=64) for c in range(CHUNKS)]
-        k_codes = [[sb.tile([P, CHUNK], U16, name=f"k_codes{c}_{o}", align_bytes=64) for o in range(PASSES)] for c in range(CHUNKS)]
-        scores = [ps.tile([P, CHUNK], F32, name=f"scores{c}") for c in range(CHUNKS)]
+        listed = [sb.tile([P, GATHER], U32, name=f"listed{c}", align_bytes=64) for c in range(N // GATHER)]
+        scores = [ps.tile([P, w], F32, name=f"scores{i}") for i, w in enumerate(WIDTHS)]
 
-        def cast(o):
+        for c in range(N // GATHER):
+            cols = GATHER // 16
+            nc.vector.tensor_copy(listed[c][:], word_pool[:].indirect(offsets[:, c * cols : (c + 1) * cols]))
+        for o in range(PASSES):
             nc.scalar.activation(q_bf[o][:], q_raw[o][:].rearrange("p j q -> p q j"), ACT.Copy)
+
+        k_first = sb.tile([P, PASSES * WIDTHS[0]], U16, name="k_first", tag="after_cast0", align_bytes=64)
+        k_rest = sb.tile([P, PASSES * (N - WIDTHS[0])], U16, name="k_rest", tag="after_cast1", align_bytes=64)
+
+        def k_codes(i):
+            if i == 0:
+                flat = k_first[:]
+            else:
+                lo = PASSES * (STARTS[i] - WIDTHS[0])
+                flat = k_rest[:, lo : lo + PASSES * WIDTHS[i]]
+            return flat.rearrange("p (o n) -> p o n", o=PASSES)
 
         def quantise(o):
             nc.vector.quantize_mx(out=q_codes[o][:].bitcast(FP8X4), scales=q_planes[o][:], in_=q_bf[o][:].rearrange("p q j -> p (q j)"))
 
-        def gather(c):
-            cols = CHUNK // 16
-            nc.vector.tensor_copy(listed[c][:], word_pool[:].indirect(offsets[:, c * cols : (c + 1) * cols]))
+        def part(i):
+            c, lo = divmod(STARTS[i], GATHER)
+            halves = listed[c][:, lo : lo + WIDTHS[i]].bitcast(U16).rearrange("p (n o) -> p o n", o=PASSES)
+            nc.vector.tensor_copy(k_codes(i), halves)
 
-        def part(c, o):
-            halves = listed[c][:].bitcast(U16).rearrange("p (n o) -> p o n", o=PASSES)
-            nc.vector.tensor_copy(k_codes[c][o][:], halves[:, o, :])
+        def multiply(i):
+            width = 512 if WIDTHS[i] == 512 else GROUP
+            for lo in range(0, WIDTHS[i], width):
+                for o in range(PASSES):
+                    nc.tensor.matmul_mx(
+                        out=scores[i][:, lo : lo + width],
+                        lhsT=q_codes[o][:].bitcast(FP8X4),
+                        lhsT_scale=q_planes[o][:],
+                        rhs=k_codes(i)[:, o, lo : lo + width].bitcast(FP4X4),
+                        rhs_scale=k_planes[:, o, STARTS[i] + lo : STARTS[i] + lo + width],
+                        start=(o == 0),
+                        stop=(o == PASSES - 1),
+                    )
 
-        def multiply(c, o):
-            nc.tensor.matmul_mx(
-                out=scores[c][:],
-                lhsT=q_codes[o][:].bitcast(FP8X4),
-                lhsT_scale=q_planes[o][:],
-                rhs=k_codes[c][o][:].bitcast(FP4X4),
-                rhs_scale=k_planes[:, o, c * CHUNK : (c + 1) * CHUNK],
-                start=(o == 0),
-                stop=(o == PASSES - 1),
-            )
-
-        neg_peak = sb.tile([P, PAGES + 1], F32, name="neg_peak")
-        neg_max = sb.tile([P, 1], F32, name="neg_max")
-        sums = sb.tile([P, CHUNKS], F32, name="sums")
-        weights = [sb.tile([P, CHUNK], F32, name=f"weights{c}") for c in range(CHUNKS)]
-        peak = sb.tile([P, PAGES + 1], F32, name="peak")
+        neg_peak = sb.tile([P, PAGES + PIECES], F32, name="neg_peak")
+        sums = sb.tile([P, PIECES], F32, name="sums")
+        weights = [sb.tile([P, w], F32, name=f"weights{i}") for i, w in enumerate(WIDTHS)]
+        peak = sb.tile([P, PAGES + PIECES], F32, name="peak")
+        scaled = sb.tile([P, PIECES], F32, name="scaled")
         total = sb.tile([P, 1], F32, name="total")
         inverse = sb.tile([P, 1], F32, name="inverse")
         result = sb.tile([P, PAGES], F32, name="result")
 
-        def page_peaks(c):
-            nc.vector.tensor_reduce(
-                neg_peak[:, c * CHUNK_PAGES : (c + 1) * CHUNK_PAGES],
-                scores[c][:].rearrange("p (j s) -> p j s", s=SEG),
-                AX.X,
-                ALU.max,
-                negate=True,
-            )
+        def pages(i):
+            return slice(STARTS[i] // SEG, (STARTS[i] + WIDTHS[i]) // SEG)
 
-        identity = sb.tile([P, P], BF16, name="identity")
-        make_identity(nc, identity[:])
-        idle = [ps.tile([P, 8, P], BF16, name=f"idle{b}") for b in range(6)]
-        for i in range(WARM_UP):
-            nc.tensor.transpose(idle[i % 6][:, (i // 6) % 8, :], identity[:], identity[:])
+        def page_peaks(i):
+            nc.vector.tensor_reduce(neg_peak[:, pages(i)], scores[i][:].rearrange("p (j s) -> p j s", s=SEG), AX.X, ALU.max, negate=True)
 
-        cast(0)
-        cast(1)
-        q_cols = q_bf[0][:].rearrange("p q j -> p (q j)")
-        for i in range(WARM_UP, WARM_UP + BRIDGE):
-            nc.tensor.transpose(idle[i % 6][:, (i // 6) % 8, :], q_cols[:, (i % 4) * P : (i % 4 + 1) * P], identity[:])
-        gather(0)
-        part(0, 0)
-        gather(1)
+        def weigh(i, shift):
+            nc.scalar.activation(weights[i][:], scores[i][:], ACT.Exp, bias=shift, accum_out=sums[:, i : i + 1])
+
         quantise(0)
-        part(0, 1)
+        part(0)
         quantise(1)
-        multiply(0, 0)
-        multiply(0, 1)
-        part(1, 0)
-        part(1, 1)
-        multiply(1, 0)
-        multiply(1, 1)
+        multiply(0)
+        for i in range(1, PIECES):
+            part(i)
+            multiply(i)
 
-        page_peaks(0)
-        nc.vector.tensor_reduce(neg_peak[:, PAGES : PAGES + 1], neg_peak[:, 0:CHUNK_PAGES], AX.X, ALU.min)
-        nc.scalar.activation(weights[0][:], scores[0][:], ACT.Exp, bias=neg_peak[:, PAGES : PAGES + 1], accum_out=sums[:, 0:1])
-        page_peaks(1)
-        nc.vector.tensor_reduce(neg_max[:], neg_peak[:, 0:PAGES], AX.X, ALU.min)
-        nc.scalar.activation(peak[:], neg_peak[:], ACT.Exp, bias=neg_max[:], scale=-1.0)
-        nc.scalar.activation(weights[1][:], scores[1][:], ACT.Exp, bias=neg_max[:], accum_out=sums[:, 1:2])
-        nc.vector.tensor_scalar(total[:], sums[:, 0:1], peak[:, PAGES : PAGES + 1], sums[:, 1:2], ALU.mult, ALU.add)
+        for i in range(LAST):
+            page_peaks(i)
+            own = neg_peak[:, PAGES + i : PAGES + i + 1]
+            nc.vector.tensor_reduce(own, neg_peak[:, pages(i)], AX.X, ALU.min)
+            weigh(i, own)
+        page_peaks(LAST)
+        neg_max = neg_peak[:, PAGES + LAST :]
+        nc.vector.tensor_reduce(neg_max, neg_peak[:, pages(LAST).start : PAGES + LAST], AX.X, ALU.min)
+        nc.scalar.activation(peak[:], neg_peak[:], ACT.Exp, bias=neg_max, scale=-1.0)
+        weigh(LAST, neg_max)
+        nc.vector.scalar_tensor_tensor(scaled[:], sums[:], 1.0, peak[:, PAGES:], ALU.mult, ALU.mult, accum_out=total[:])
         nc.vector.reciprocal(inverse[:], total[:])
         nc.vector.tensor_scalar(result[:], peak[:, 0:PAGES], inverse[:], None, ALU.mult)
         nc.sync.dma_start(out[0], result[:])

@@ -23,7 +23,9 @@ K_PASS = P * PACK
 PASSES = D // K_PASS
 GATHER = 512
 GROUP = 128
-WIDTHS = (256, 256, 256, 128, 128)
+HEAD = 256
+PART = 256
+WIDTHS = (128, 128, 256, 256, 128, 128)
 STARTS = tuple(sum(WIDTHS[:i]) for i in range(len(WIDTHS)))
 PIECES = len(WIDTHS)
 LAST = PIECES - 1
@@ -70,40 +72,36 @@ def tile_attend_page_peak_kernel(tc, qT, k_words, k_scales, offs, out):
             cols = GATHER // 16
             nc.vector.tensor_copy(listed[c][:], word_pool[:].indirect(offsets[:, c * cols : (c + 1) * cols]))
         for o in range(PASSES):
-            nc.scalar.activation(q_bf[o][:], q_raw[o][:].rearrange("p j q -> p q j"), ACT.Copy)
+            nc.scalar.activation(q_bf[o][:].rearrange("p (c i) j -> p c j i", i=4), q_raw[o][:].rearrange("p j (c i) -> p c j i", i=4), ACT.Copy)
 
-        k_first = sb.tile([P, PASSES * WIDTHS[0]], U16, name="k_first", tag="after_cast0", align_bytes=64)
-        k_rest = sb.tile([P, PASSES * (N - WIDTHS[0])], U16, name="k_rest", tag="after_cast1", align_bytes=64)
+        k_first = sb.tile([P, HEAD], U16, name="k_first", tag="after_cast0", align_bytes=64)
+        k_rest = sb.tile([P, PASSES * N - HEAD], U16, name="k_rest", tag="after_cast1", align_bytes=64)
 
-        def k_codes(i):
-            if i == 0:
-                flat = k_first[:]
-            else:
-                lo = PASSES * (STARTS[i] - WIDTHS[0])
-                flat = k_rest[:, lo : lo + PASSES * WIDTHS[i]]
-            return flat.rearrange("p (o n) -> p o n", o=PASSES)
+        def k_codes(slot, o, width):
+            if slot < HEAD:
+                return (k_first, k_rest)[o][:, slot : slot + width]
+            part_start = slot - (slot - HEAD) % PART
+            lo = HEAD + PASSES * (part_start - HEAD) + o * PART + slot - part_start
+            return k_rest[:, lo : lo + width]
 
         def quantise(o):
             nc.vector.quantize_mx(out=q_codes[o][:].bitcast(FP8X4), scales=q_planes[o][:], in_=q_bf[o][:].rearrange("p q j -> p (q j)"))
 
-        def part(i):
-            c, lo = divmod(STARTS[i], GATHER)
-            halves = listed[c][:, lo : lo + WIDTHS[i]].bitcast(U16).rearrange("p (n o) -> p o n", o=PASSES)
-            nc.vector.tensor_copy(k_codes(i), halves)
+        def halves(slot, width):
+            c, lo = divmod(slot, GATHER)
+            return listed[c][:, lo : lo + width].bitcast(U16).rearrange("p (n o) -> p o n", o=PASSES)
 
-        def multiply(i):
-            width = 512 if WIDTHS[i] == 512 else GROUP
-            for lo in range(0, WIDTHS[i], width):
-                for o in range(PASSES):
-                    nc.tensor.matmul_mx(
-                        out=scores[i][:, lo : lo + width],
-                        lhsT=q_codes[o][:].bitcast(FP8X4),
-                        lhsT_scale=q_planes[o][:],
-                        rhs=k_codes(i)[:, o, lo : lo + width].bitcast(FP4X4),
-                        rhs_scale=k_planes[:, o, STARTS[i] + lo : STARTS[i] + lo + width],
-                        start=(o == 0),
-                        stop=(o == PASSES - 1),
-                    )
+        def multiply(slot, o):
+            i = max(n for n in range(PIECES) if STARTS[n] <= slot)
+            nc.tensor.matmul_mx(
+                out=scores[i][:, slot - STARTS[i] : slot - STARTS[i] + GROUP],
+                lhsT=q_codes[o][:].bitcast(FP8X4),
+                lhsT_scale=q_planes[o][:],
+                rhs=k_codes(slot, o, GROUP).bitcast(FP4X4),
+                rhs_scale=k_planes[:, o, slot : slot + GROUP],
+                start=(o == 0),
+                stop=(o == PASSES - 1),
+            )
 
         neg_peak = sb.tile([P, PAGES + PIECES], F32, name="neg_peak")
         sums = sb.tile([P, PIECES], F32, name="sums")
@@ -123,13 +121,16 @@ def tile_attend_page_peak_kernel(tc, qT, k_words, k_scales, offs, out):
         def weigh(i, shift):
             nc.scalar.activation(weights[i][:], scores[i][:], ACT.Exp, bias=shift, accum_out=sums[:, i : i + 1])
 
-        quantise(0)
-        part(0)
-        quantise(1)
-        multiply(0)
-        for i in range(1, PIECES):
-            part(i)
-            multiply(i)
+        for o in range(PASSES):
+            quantise(o)
+            nc.vector.tensor_copy(k_codes(0, o, HEAD), halves(0, HEAD)[:, o, :])
+            for slot in range(0, HEAD, GROUP):
+                multiply(slot, o)
+        for start in range(HEAD, N, PART):
+            nc.vector.tensor_copy(k_codes(start, 0, PASSES * PART).rearrange("p (o n) -> p o n", o=PASSES), halves(start, PART))
+            for slot in range(start, start + PART, GROUP):
+                for o in range(PASSES):
+                    multiply(slot, o)
 
         for i in range(LAST):
             page_peaks(i)

@@ -18,9 +18,13 @@ ALU = mybir.AluOpType
 AX = mybir.AxisListType
 
 P = 128
+QUADRANT = 32
 PACK = 4
 K_PASS = P * PACK
 PASSES = D // K_PASS
+BLOCKS = 4
+STRIPE = 16
+LINE = 4
 GATHER = 512
 GROUP = 128
 HEAD = 256
@@ -38,28 +42,29 @@ def tile_attend_page_peak_kernel(tc, qT, k_words, k_scales, offs, out):
         sb = ctx.enter_context(tc.tile_pool(name="sb", bufs=1))
         ps = ctx.enter_context(tc.psum_pool(name="ps", bufs=1))
 
-        offsets = sb.tile([P, N // 16], U16, name="offsets")
+        offsets = sb.tile([P, N // STRIPE], U16, name="offsets")
         word_pool = sb.tile([P, T], U32, name="word_pool", align_bytes=64)
         byte_pool = sb.tile([P, T], U8, name="byte_pool", align_bytes=64)
         byte_listed = sb.tile([P, N], U8, name="byte_listed", align_bytes=64)
         k_planes = sb.tile([P, PASSES, N], U8, name="k_planes", align_bytes=64)
 
-        nc.vector.memset(byte_pool[32:64, :].bitcast(I32), 0)
-        nc.vector.memset(byte_pool[64:P, :].bitcast(I32), 0)
+        nc.vector.memset(byte_pool[QUADRANT : 2 * QUADRANT, :].bitcast(I32), 0)
+        nc.vector.memset(byte_pool[2 * QUADRANT : P, :].bitcast(I32), 0)
         nc.vector.memset(k_planes[:].rearrange("p o n -> p (o n)").bitcast(I32), 0)
 
+        nc.sync.dma_start(byte_pool[0:QUADRANT, :].bitcast(I32), k_scales.rearrange("o f t -> f o t").bitcast(I32))
         nc.sync.dma_start(offsets[:], offs)
-        nc.sync.dma_start(byte_pool[0:32, :].bitcast(I32), k_scales.rearrange("o f t -> f o t").bitcast(I32))
         nc.sync.dma_start(word_pool[:].bitcast(I32), k_words[0].rearrange("p t b -> p (t b)").bitcast(I32))
         q_raw = [sb.tile([P, PACK, NQ], F32, name=f"q_raw{o}", tag=f"after_cast{o}", align_bytes=64) for o in range(PASSES)]
         for o in range(PASSES):
             nc.sync.dma_start(q_raw[o][:], qT[0, o * K_PASS : (o + 1) * K_PASS, :].rearrange("(p j) q -> p j q", j=PACK))
 
         nc.vector.tensor_copy(byte_listed[:], byte_pool[:].indirect(offsets[:]))
+        rows = BLOCKS * PASSES
         for quad in (0, 2, 1, 3):
             nc.sync.dma_start(
-                k_planes[32 * quad : 32 * quad + 4, :, :].rearrange("p o n -> p (o n)").bitcast(I32),
-                byte_listed[8 * quad : 8 * quad + 8, :].bitcast(I32),
+                k_planes[QUADRANT * quad : QUADRANT * quad + BLOCKS, :, :].rearrange("p o n -> p (o n)").bitcast(I32),
+                byte_listed[rows * quad : rows * (quad + 1), :].bitcast(I32),
             )
 
         q_bf = [sb.tile([P, NQ, PACK], BF16, name=f"q_bf{o}", align_bytes=64) for o in range(PASSES)]
@@ -68,11 +73,14 @@ def tile_attend_page_peak_kernel(tc, qT, k_words, k_scales, offs, out):
         listed = [sb.tile([P, GATHER], U32, name=f"listed{c}", align_bytes=64) for c in range(N // GATHER)]
         scores = [ps.tile([P, w], F32, name=f"scores{i}") for i, w in enumerate(WIDTHS)]
 
+        cols = GATHER // STRIPE
         for c in range(N // GATHER):
-            cols = GATHER // 16
             nc.vector.tensor_copy(listed[c][:], word_pool[:].indirect(offsets[:, c * cols : (c + 1) * cols]))
+
         for o in range(PASSES):
-            nc.scalar.activation(q_bf[o][:].rearrange("p (c i) j -> p c j i", i=4), q_raw[o][:].rearrange("p j (c i) -> p c j i", i=4), ACT.Copy)
+            nc.scalar.activation(
+                q_bf[o][:].rearrange("p (c i) j -> p c j i", i=LINE), q_raw[o][:].rearrange("p j (c i) -> p c j i", i=LINE), ACT.Copy
+            )
 
         k_first = sb.tile([P, HEAD], U16, name="k_first", tag="after_cast0", align_bytes=64)
         k_rest = sb.tile([P, PASSES * N - HEAD], U16, name="k_rest", tag="after_cast1", align_bytes=64)
@@ -137,6 +145,7 @@ def tile_attend_page_peak_kernel(tc, qT, k_words, k_scales, offs, out):
             own = neg_peak[:, PAGES + i : PAGES + i + 1]
             nc.vector.tensor_reduce(own, neg_peak[:, pages(i)], AX.X, ALU.min)
             weigh(i, own)
+
         page_peaks(LAST)
         neg_max = neg_peak[:, PAGES + LAST :]
         nc.vector.tensor_reduce(neg_max, neg_peak[:, pages(LAST).start : PAGES + LAST], AX.X, ALU.min)

@@ -27,9 +27,9 @@ STRIPE = 16
 LINE = 4
 GATHER = 512
 GROUP = 128
-HEAD = 256
-PART = 256
-WIDTHS = (128, 128, 256, 256, 128, 128)
+HEAD = 384
+PART_STARTS = (HEAD, 512, 768, N)
+WIDTHS = (128, 128, 256, 128, 128, 128, 128)
 STARTS = tuple(sum(WIDTHS[:i]) for i in range(len(WIDTHS)))
 PIECES = len(WIDTHS)
 LAST = PIECES - 1
@@ -82,14 +82,18 @@ def tile_attend_page_peak_kernel(tc, qT, k_words, k_scales, offs, out):
                 q_bf[o][:].rearrange("p (c i) j -> p c j i", i=LINE), q_raw[o][:].rearrange("p j (c i) -> p c j i", i=LINE), ACT.Copy
             )
 
-        k_first = sb.tile([P, HEAD], U16, name="k_first", tag="after_cast0", align_bytes=64)
-        k_rest = sb.tile([P, PASSES * N - HEAD], U16, name="k_rest", tag="after_cast1", align_bytes=64)
+        k_head = [
+            sb.tile([P, HEAD], U16, name="k_head0", align_bytes=64),
+            sb.tile([P, HEAD], U16, name="k_head1", tag="after_cast0", align_bytes=64),
+        ]
+        k_rest = sb.tile([P, PASSES * (N - HEAD)], U16, name="k_rest", tag="after_cast1", align_bytes=64)
 
         def k_codes(slot, o, width):
             if slot < HEAD:
-                return (k_first, k_rest)[o][:, slot : slot + width]
-            part_start = slot - (slot - HEAD) % PART
-            lo = HEAD + PASSES * (part_start - HEAD) + o * PART + slot - part_start
+                return k_head[o][:, slot : slot + width]
+            part_start = max(a for a in PART_STARTS if a <= slot)
+            part_stop = min(a for a in PART_STARTS if a > slot)
+            lo = PASSES * (part_start - HEAD) + o * (part_stop - part_start) + slot - part_start
             return k_rest[:, lo : lo + width]
 
         def quantise(o):
@@ -130,25 +134,29 @@ def tile_attend_page_peak_kernel(tc, qT, k_words, k_scales, offs, out):
             nc.scalar.activation(weights[i][:], scores[i][:], ACT.Exp, bias=shift, accum_out=sums[:, i : i + 1])
 
         for o in range(PASSES):
-            quantise(o)
             nc.vector.tensor_copy(k_codes(0, o, HEAD), halves(0, HEAD)[:, o, :])
+            quantise(o)
             for slot in range(0, HEAD, GROUP):
                 multiply(slot, o)
-        for start in range(HEAD, N, PART):
-            nc.vector.tensor_copy(k_codes(start, 0, PASSES * PART).rearrange("p (o n) -> p o n", o=PASSES), halves(start, PART))
-            for slot in range(start, start + PART, GROUP):
+        for start, stop in zip(PART_STARTS, PART_STARTS[1:]):
+            width = stop - start
+            nc.vector.tensor_copy(k_codes(start, 0, PASSES * width).rearrange("p (o n) -> p o n", o=PASSES), halves(start, width))
+            for slot in range(start, stop, GROUP):
                 for o in range(PASSES):
                     multiply(slot, o)
 
-        for i in range(LAST):
-            page_peaks(i)
+        def piece_peak(i):
             own = neg_peak[:, PAGES + i : PAGES + i + 1]
             nc.vector.tensor_reduce(own, neg_peak[:, pages(i)], AX.X, ALU.min)
             weigh(i, own)
 
-        page_peaks(LAST)
+        for i in range(PIECES):
+            page_peaks(i)
+            if i > 0:
+                piece_peak(i - 1)
+
         neg_max = neg_peak[:, PAGES + LAST :]
-        nc.vector.tensor_reduce(neg_max, neg_peak[:, pages(LAST).start : PAGES + LAST], AX.X, ALU.min)
+        nc.vector.tensor_reduce(neg_max, neg_peak[:, pages(LAST - 1).start : PAGES + LAST - 1], AX.X, ALU.min)
         nc.scalar.activation(peak[:], neg_peak[:], ACT.Exp, bias=neg_max, scale=-1.0)
         weigh(LAST, neg_max)
         nc.vector.scalar_tensor_tensor(scaled[:], sums[:], 1.0, peak[:, PAGES:], ALU.mult, ALU.mult, accum_out=total[:])

@@ -45,12 +45,13 @@ def tile_attend_page_peak_kernel(tc, qT, k_words, k_scales, offs, out):
         offsets = sb.tile([P, N // STRIPE], U16, name="offsets")
         word_pool = sb.tile([P, T], U32, name="word_pool", align_bytes=64)
         byte_pool = sb.tile([P, T], U8, name="byte_pool", align_bytes=64)
-        byte_listed = sb.tile([P, N], U8, name="byte_listed", align_bytes=64)
-        k_planes = sb.tile([P, PASSES, N], U8, name="k_planes", align_bytes=64)
+        byte_listed = [sb.tile([P, GATHER], U8, name=f"byte_listed{c}", align_bytes=64) for c in range(N // GATHER)]
+        k_planes = [sb.tile([P, PASSES, GATHER], U8, name=f"k_planes{c}", align_bytes=64) for c in range(N // GATHER)]
 
         nc.vector.memset(byte_pool[QUADRANT : 2 * QUADRANT, :].bitcast(I32), 0)
         nc.vector.memset(byte_pool[2 * QUADRANT : P, :].bitcast(I32), 0)
-        nc.vector.memset(k_planes[:].rearrange("p o n -> p (o n)").bitcast(I32), 0)
+        for planes in k_planes:
+            nc.vector.memset(planes[:].rearrange("p o n -> p (o n)").bitcast(I32), 0)
 
         nc.sync.dma_start(byte_pool[0:QUADRANT, :].bitcast(I32), k_scales.rearrange("o f t -> f o t").bitcast(I32))
         nc.sync.dma_start(offsets[:], offs)
@@ -59,13 +60,15 @@ def tile_attend_page_peak_kernel(tc, qT, k_words, k_scales, offs, out):
         for o in range(PASSES):
             nc.sync.dma_start(q_raw[o][:], qT[0, o * K_PASS : (o + 1) * K_PASS, :].rearrange("(p j) q -> p j q", j=PACK))
 
-        nc.vector.tensor_copy(byte_listed[:], byte_pool[:].indirect(offsets[:]))
+        cols = GATHER // STRIPE
         rows = BLOCKS * PASSES
-        for quad in (0, 2, 1, 3):
-            nc.sync.dma_start(
-                k_planes[QUADRANT * quad : QUADRANT * quad + BLOCKS, :, :].rearrange("p o n -> p (o n)").bitcast(I32),
-                byte_listed[rows * quad : rows * (quad + 1), :].bitcast(I32),
-            )
+        for c in range(N // GATHER):
+            nc.vector.tensor_copy(byte_listed[c][:], byte_pool[:].indirect(offsets[:, c * cols : (c + 1) * cols]))
+            for quad in (0, 2, 1, 3):
+                nc.sync.dma_start(
+                    k_planes[c][QUADRANT * quad : QUADRANT * quad + BLOCKS, :, :].rearrange("p o n -> p (o n)").bitcast(I32),
+                    byte_listed[c][rows * quad : rows * (quad + 1), :].bitcast(I32),
+                )
 
         q_bf = [sb.tile([P, NQ, PACK], BF16, name=f"q_bf{o}", align_bytes=64) for o in range(PASSES)]
         q_codes = [sb.tile([P, NQ], U32, name=f"q_codes{o}", align_bytes=64) for o in range(PASSES)]
@@ -73,7 +76,6 @@ def tile_attend_page_peak_kernel(tc, qT, k_words, k_scales, offs, out):
         listed = [sb.tile([P, GATHER], U32, name=f"listed{c}", align_bytes=64) for c in range(N // GATHER)]
         scores = [ps.tile([P, w], F32, name=f"scores{i}") for i, w in enumerate(WIDTHS)]
 
-        cols = GATHER // STRIPE
         for c in range(N // GATHER):
             nc.vector.tensor_copy(listed[c][:], word_pool[:].indirect(offsets[:, c * cols : (c + 1) * cols]))
 
@@ -110,7 +112,7 @@ def tile_attend_page_peak_kernel(tc, qT, k_words, k_scales, offs, out):
                 lhsT=q_codes[o][:].bitcast(FP8X4),
                 lhsT_scale=q_planes[o][:],
                 rhs=k_codes(slot, o, GROUP).bitcast(FP4X4),
-                rhs_scale=k_planes[:, o, slot : slot + GROUP],
+                rhs_scale=k_planes[slot // GATHER][:, o, slot % GATHER : slot % GATHER + GROUP],
                 start=(o == 0),
                 stop=(o == PASSES - 1),
             )

@@ -19,6 +19,7 @@ AX = mybir.AxisListType
 
 P = 128
 QUADRANT = 32
+ROW0 = P - QUADRANT
 PACK = 4
 K_PASS = P * PACK
 PASSES = D // K_PASS
@@ -48,12 +49,11 @@ def tile_attend_page_peak_kernel(tc, qT, k_words, k_scales, offs, out):
         byte_listed = [sb.tile([P, GATHER], U8, name=f"byte_listed{c}", align_bytes=64) for c in range(N // GATHER)]
         k_planes = [sb.tile([P, PASSES, GATHER], U8, name=f"k_planes{c}", align_bytes=64) for c in range(N // GATHER)]
 
-        nc.vector.memset(byte_pool[QUADRANT : 2 * QUADRANT, :].bitcast(I32), 0)
-        nc.vector.memset(byte_pool[2 * QUADRANT : P, :].bitcast(I32), 0)
+        nc.vector.memset(byte_pool[0:ROW0, :].bitcast(I32), 0)
         for planes in k_planes:
             nc.vector.memset(planes[:].rearrange("p o n -> p (o n)").bitcast(I32), 0)
 
-        nc.sync.dma_start(byte_pool[0:QUADRANT, :].bitcast(I32), k_scales.rearrange("o f t -> f o t").bitcast(I32))
+        nc.sync.dma_start(byte_pool[ROW0:P, :].bitcast(I32), k_scales.rearrange("o f t -> f o t").bitcast(I32))
         nc.sync.dma_start(offsets[:], offs)
         nc.sync.dma_start(word_pool[:].bitcast(I32), k_words[0].rearrange("p t b -> p (t b)").bitcast(I32))
         q_raw = [sb.tile([P, PACK, NQ], F32, name=f"q_raw{o}", tag=f"after_cast{o}", align_bytes=64) for o in range(PASSES)]
@@ -67,7 +67,7 @@ def tile_attend_page_peak_kernel(tc, qT, k_words, k_scales, offs, out):
             for quad in (0, 2, 1, 3):
                 nc.sync.dma_start(
                     k_planes[c][QUADRANT * quad : QUADRANT * quad + BLOCKS, :, :].rearrange("p o n -> p (o n)").bitcast(I32),
-                    byte_listed[c][rows * quad : rows * (quad + 1), :].bitcast(I32),
+                    byte_listed[c][ROW0 + rows * quad : ROW0 + rows * (quad + 1), :].bitcast(I32),
                 )
 
         q_bf = [sb.tile([P, NQ, PACK], BF16, name=f"q_bf{o}", align_bytes=64) for o in range(PASSES)]

@@ -28,9 +28,9 @@ STRIPE = 16
 LINE = 4
 GATHER = 512
 GROUP = 128
-HEAD = 384
-PART_STARTS = (HEAD, 512, 768, N)
-WIDTHS = (128, 128, 256, 128, 128, 128, 128)
+HEAD = 512
+PART_STARTS = (HEAD, 768, N)
+WIDTHS = (128,) * 8
 STARTS = tuple(sum(WIDTHS[:i]) for i in range(len(WIDTHS)))
 PIECES = len(WIDTHS)
 LAST = PIECES - 1
@@ -135,9 +135,13 @@ def tile_attend_page_peak_kernel(tc, qT, k_words, k_scales, offs, out):
         def weigh(i, shift):
             nc.scalar.activation(weights[i][:], scores[i][:], ACT.Exp, bias=shift, accum_out=sums[:, i : i + 1])
 
+        half = HEAD // 2
+        nc.vector.tensor_copy(k_codes(0, 0, half), halves(0, half)[:, 0, :])
+        quantise(0)
+        nc.vector.tensor_copy(k_codes(half, 0, half), halves(half, half)[:, 0, :])
+        nc.vector.tensor_copy(k_codes(0, 1, HEAD), halves(0, HEAD)[:, 1, :])
+        quantise(1)
         for o in range(PASSES):
-            nc.vector.tensor_copy(k_codes(0, o, HEAD), halves(0, HEAD)[:, o, :])
-            quantise(o)
             for slot in range(0, HEAD, GROUP):
                 multiply(slot, o)
         for start, stop in zip(PART_STARTS, PART_STARTS[1:]):

@@ -29,6 +29,8 @@ LINE = 4
 GATHER = 512
 GROUP = 128
 HEAD = 512
+FIRST = 256
+SECOND = 256
 PART_STARTS = (HEAD, 768, N)
 WIDTHS = (128,) * 8
 STARTS = tuple(sum(WIDTHS[:i]) for i in range(len(WIDTHS)))
@@ -84,19 +86,32 @@ def tile_attend_page_peak_kernel(tc, qT, k_words, k_scales, offs, out):
                 q_bf[o][:].rearrange("p (c i) j -> p c j i", i=LINE), q_raw[o][:].rearrange("p j (c i) -> p c j i", i=LINE), ACT.Copy
             )
 
-        k_head = [
-            sb.tile([P, HEAD], U16, name="k_head0", align_bytes=64),
-            sb.tile([P, HEAD], U16, name="k_head1", tag="after_cast0", align_bytes=64),
-        ]
-        k_rest = sb.tile([P, PASSES * (N - HEAD)], U16, name="k_rest", tag="after_cast1", align_bytes=64)
+        runs = (
+            ((0, 0, FIRST),),
+            ((0, FIRST, HEAD - FIRST), (1, 0, SECOND)),
+            ((1, SECOND, HEAD - SECOND),) + tuple((None, a, b - a) for a, b in zip(PART_STARTS, PART_STARTS[1:])),
+        )
+        place = {}
+        for n, group in enumerate(runs):
+            width = sum(w * (PASSES if o is None else 1) for o, a, w in group)
+            tag = f"after_cast{n - 1}" if n else "k_first"
+            tile = sb.tile([P, width], U16, name=f"k_codes{n}", tag=tag, align_bytes=64)
+            lo = 0
+            for o, a, w in group:
+                for each in range(PASSES) if o is None else (o,):
+                    for slot in range(a, a + w, GROUP):
+                        place[slot, each] = (tile, lo + slot - a)
+                    lo += w
 
         def k_codes(slot, o, width):
-            if slot < HEAD:
-                return k_head[o][:, slot : slot + width]
-            part_start = max(a for a in PART_STARTS if a <= slot)
-            part_stop = min(a for a in PART_STARTS if a > slot)
-            lo = PASSES * (part_start - HEAD) + o * (part_stop - part_start) + slot - part_start
-            return k_rest[:, lo : lo + width]
+            tile, lo = place[slot, o]
+            return tile[:, lo : lo + width]
+
+        def separate(o, slot, width):
+            if o is None:
+                nc.vector.tensor_copy(k_codes(slot, 0, PASSES * width).rearrange("p (o n) -> p o n", o=PASSES), halves(slot, width))
+            else:
+                nc.vector.tensor_copy(k_codes(slot, o, width), halves(slot, width)[:, o, :])
 
         def quantise(o):
             nc.vector.quantize_mx(out=q_codes[o][:].bitcast(FP8X4), scales=q_planes[o][:], in_=q_bf[o][:].rearrange("p q j -> p (q j)"))
@@ -135,21 +150,17 @@ def tile_attend_page_peak_kernel(tc, qT, k_words, k_scales, offs, out):
         def weigh(i, shift):
             nc.scalar.activation(weights[i][:], scores[i][:], ACT.Exp, bias=shift, accum_out=sums[:, i : i + 1])
 
-        half = HEAD // 2
-        nc.vector.tensor_copy(k_codes(0, 0, half), halves(0, half)[:, 0, :])
-        quantise(0)
-        nc.vector.tensor_copy(k_codes(half, 0, half), halves(half, half)[:, 0, :])
-        nc.vector.tensor_copy(k_codes(0, 1, HEAD), halves(0, HEAD)[:, 1, :])
-        quantise(1)
+        for n, group in enumerate(runs):
+            for run in group:
+                separate(*run)
+            if n < PASSES:
+                quantise(n)
         for o in range(PASSES):
             for slot in range(0, HEAD, GROUP):
                 multiply(slot, o)
-        for start, stop in zip(PART_STARTS, PART_STARTS[1:]):
-            width = stop - start
-            nc.vector.tensor_copy(k_codes(start, 0, PASSES * width).rearrange("p (o n) -> p o n", o=PASSES), halves(start, width))
-            for slot in range(start, stop, GROUP):
-                for o in range(PASSES):
-                    multiply(slot, o)
+        for slot in range(HEAD, N, GROUP):
+            for o in range(PASSES):
+                multiply(slot, o)
 
         def piece_peak(i):
             own = neg_peak[:, PAGES + i : PAGES + i + 1]

@@ -27,16 +27,14 @@ BLOCKS = 4
 STRIPE = 16
 LINE = 4
 GATHER = 512
-GROUP = 128
-HEAD = 512
-FIRST = 256
-SECOND = 256
-PART_STARTS = (HEAD, 768, N)
-WIDTHS = (128,) * 8
-STARTS = tuple(sum(WIDTHS[:i]) for i in range(len(WIDTHS)))
-PIECES = len(WIDTHS)
+PIECE = 128
+PIECES = N // PIECE
 LAST = PIECES - 1
+HEAD = 512
+RUN = 256
 PAGES = N // SEG
+LATE = 3
+EARLY_PAGES = (PIECES - LATE) * PIECE // SEG
 
 
 def tile_attend_page_peak_kernel(tc, qT, k_words, k_scales, offs, out):
@@ -52,15 +50,15 @@ def tile_attend_page_peak_kernel(tc, qT, k_words, k_scales, offs, out):
         k_planes = [sb.tile([P, PASSES, GATHER], U8, name=f"k_planes{c}", align_bytes=64) for c in range(N // GATHER)]
 
         nc.vector.memset(byte_pool[0:ROW0, :].bitcast(I32), 0)
-        for planes in k_planes:
-            nc.vector.memset(planes[:].rearrange("p o n -> p (o n)").bitcast(I32), 0)
+        for c in range(N // GATHER):
+            nc.vector.memset(k_planes[c][:].rearrange("p o n -> p (o n)").bitcast(I32), 0)
 
-        nc.sync.dma_start(byte_pool[ROW0:P, :].bitcast(I32), k_scales.rearrange("o f t -> f o t").bitcast(I32))
+        nc.sync.dma_start(byte_pool[ROW0:P, :].bitcast(I32), k_scales.rearrange("o f token -> f o token").bitcast(I32))
         nc.sync.dma_start(offsets[:], offs)
-        nc.sync.dma_start(word_pool[:].bitcast(I32), k_words[0].rearrange("p t b -> p (t b)").bitcast(I32))
+        nc.sync.dma_start(word_pool[:].bitcast(I32), k_words[0].rearrange("p token b -> p (token b)").bitcast(I32))
         q_raw = [sb.tile([P, PACK, NQ], F32, name=f"q_raw{o}", tag=f"after_cast{o}", align_bytes=64) for o in range(PASSES)]
         for o in range(PASSES):
-            nc.sync.dma_start(q_raw[o][:], qT[0, o * K_PASS : (o + 1) * K_PASS, :].rearrange("(p j) q -> p j q", j=PACK))
+            nc.sync.dma_start(q_raw[o][:], qT[0, o * K_PASS : (o + 1) * K_PASS, :].rearrange("(p t) q -> p t q", t=PACK))
 
         cols = GATHER // STRIPE
         rows = BLOCKS * PASSES
@@ -76,73 +74,73 @@ def tile_attend_page_peak_kernel(tc, qT, k_words, k_scales, offs, out):
         q_codes = [sb.tile([P, NQ], U32, name=f"q_codes{o}", align_bytes=64) for o in range(PASSES)]
         q_planes = [sb.tile([P, NQ], U8, name=f"q_planes{o}", align_bytes=64) for o in range(PASSES)]
         listed = [sb.tile([P, GATHER], U32, name=f"listed{c}", align_bytes=64) for c in range(N // GATHER)]
-        scores = [ps.tile([P, w], F32, name=f"scores{i}") for i, w in enumerate(WIDTHS)]
+        scores = [ps.tile([P, PIECE], F32, name=f"scores{i}") for i in range(PIECES)]
 
         for c in range(N // GATHER):
             nc.vector.tensor_copy(listed[c][:], word_pool[:].indirect(offsets[:, c * cols : (c + 1) * cols]))
 
         for o in range(PASSES):
             nc.scalar.activation(
-                q_bf[o][:].rearrange("p (c i) j -> p c j i", i=LINE), q_raw[o][:].rearrange("p j (c i) -> p c j i", i=LINE), ACT.Copy
+                q_bf[o][:].rearrange("p (r i) t -> p r t i", i=LINE), q_raw[o][:].rearrange("p t (r i) -> p r t i", i=LINE), ACT.Copy
             )
 
-        runs = (
-            ((0, 0, FIRST),),
-            ((0, FIRST, HEAD - FIRST), (1, 0, SECOND)),
-            ((1, SECOND, HEAD - SECOND),) + tuple((None, a, b - a) for a, b in zip(PART_STARTS, PART_STARTS[1:])),
+        stages = (
+            (((0,), 0),),
+            (((0,), RUN), ((1,), 0)),
+            (((1,), RUN),) + tuple(((0, 1), slot) for slot in range(HEAD, N, RUN)),
         )
+        k_codes = []
         place = {}
-        for n, group in enumerate(runs):
-            width = sum(w * (PASSES if o is None else 1) for o, a, w in group)
-            tag = f"after_cast{n - 1}" if n else "k_first"
-            tile = sb.tile([P, width], U16, name=f"k_codes{n}", tag=tag, align_bytes=64)
-            lo = 0
-            for o, a, w in group:
-                for each in range(PASSES) if o is None else (o,):
-                    for slot in range(a, a + w, GROUP):
-                        place[slot, each] = (tile, lo + slot - a)
-                    lo += w
+        for stage, runs in enumerate(stages):
+            width = RUN * sum(len(passes) for passes, first in runs)
+            tag = f"after_cast{stage - 1}" if stage else "k_first"
+            k_codes.append(sb.tile([P, width], U16, name=f"k_codes{stage}", tag=tag, align_bytes=64))
+            column = 0
+            for passes, first in runs:
+                for o in passes:
+                    for slot in range(first, first + RUN, PIECE):
+                        place[slot, o] = (stage, column)
+                        column += PIECE
 
-        def k_codes(slot, o, width):
-            tile, lo = place[slot, o]
-            return tile[:, lo : lo + width]
-
-        def separate(o, slot, width):
-            if o is None:
-                nc.vector.tensor_copy(k_codes(slot, 0, PASSES * width).rearrange("p (o n) -> p o n", o=PASSES), halves(slot, width))
+        def separate(passes, first):
+            stage, column = place[first, passes[0]]
+            target = k_codes[stage][:, column : column + len(passes) * RUN]
+            c, lo = divmod(first, GATHER)
+            both = listed[c][:, lo : lo + RUN].bitcast(U16).rearrange("p (n o) -> p o n", o=PASSES)
+            if len(passes) == PASSES:
+                nc.vector.tensor_copy(target.rearrange("p (o n) -> p o n", o=PASSES), both)
             else:
-                nc.vector.tensor_copy(k_codes(slot, o, width), halves(slot, width)[:, o, :])
+                nc.vector.tensor_copy(target, both[:, passes[0], :])
 
         def quantise(o):
-            nc.vector.quantize_mx(out=q_codes[o][:].bitcast(FP8X4), scales=q_planes[o][:], in_=q_bf[o][:].rearrange("p q j -> p (q j)"))
-
-        def halves(slot, width):
-            c, lo = divmod(slot, GATHER)
-            return listed[c][:, lo : lo + width].bitcast(U16).rearrange("p (n o) -> p o n", o=PASSES)
+            nc.vector.quantize_mx(out=q_codes[o][:].bitcast(FP8X4), scales=q_planes[o][:], in_=q_bf[o][:].rearrange("p q t -> p (q t)"))
 
         def multiply(slot, o):
-            i = max(n for n in range(PIECES) if STARTS[n] <= slot)
+            stage, column = place[slot, o]
+            c, lo = divmod(slot, GATHER)
             nc.tensor.matmul_mx(
-                out=scores[i][:, slot - STARTS[i] : slot - STARTS[i] + GROUP],
+                out=scores[slot // PIECE][:],
                 lhsT=q_codes[o][:].bitcast(FP8X4),
                 lhsT_scale=q_planes[o][:],
-                rhs=k_codes(slot, o, GROUP).bitcast(FP4X4),
-                rhs_scale=k_planes[slot // GATHER][:, o, slot % GATHER : slot % GATHER + GROUP],
+                rhs=k_codes[stage][:, column : column + PIECE].bitcast(FP4X4),
+                rhs_scale=k_planes[c][:, o, lo : lo + PIECE],
                 start=(o == 0),
                 stop=(o == PASSES - 1),
             )
 
-        neg_peak = sb.tile([P, PAGES + PIECES], F32, name="neg_peak")
+        neg_peak = sb.tile([P, PIECES + EARLY_PAGES], F32, name="neg_peak")
+        neg_max = sb.tile([P, 1], F32, name="neg_max")
+        late_peak = sb.tile([P, LATE, PIECE // SEG], F32, name="late_peak")
         sums = sb.tile([P, PIECES], F32, name="sums")
-        weights = [sb.tile([P, w], F32, name=f"weights{i}") for i, w in enumerate(WIDTHS)]
-        peak = sb.tile([P, PAGES + PIECES], F32, name="peak")
+        weights = [sb.tile([P, PIECE], F32, name=f"weights{i}") for i in range(PIECES)]
+        peak = sb.tile([P, PIECES + PAGES], F32, name="peak")
         scaled = sb.tile([P, PIECES], F32, name="scaled")
         total = sb.tile([P, 1], F32, name="total")
         inverse = sb.tile([P, 1], F32, name="inverse")
         result = sb.tile([P, PAGES], F32, name="result")
 
         def pages(i):
-            return slice(STARTS[i] // SEG, (STARTS[i] + WIDTHS[i]) // SEG)
+            return slice(PIECES + i * PIECE // SEG, PIECES + (i + 1) * PIECE // SEG)
 
         def page_peaks(i):
             nc.vector.tensor_reduce(neg_peak[:, pages(i)], scores[i][:].rearrange("p (j s) -> p j s", s=SEG), AX.X, ALU.max, negate=True)
@@ -150,33 +148,44 @@ def tile_attend_page_peak_kernel(tc, qT, k_words, k_scales, offs, out):
         def weigh(i, shift):
             nc.scalar.activation(weights[i][:], scores[i][:], ACT.Exp, bias=shift, accum_out=sums[:, i : i + 1])
 
-        for n, group in enumerate(runs):
-            for run in group:
-                separate(*run)
-            if n < PASSES:
-                quantise(n)
+        for stage, runs in enumerate(stages):
+            for passes, first in runs:
+                separate(passes, first)
+            if stage < PASSES:
+                quantise(stage)
         for o in range(PASSES):
-            for slot in range(0, HEAD, GROUP):
+            for slot in range(0, HEAD, PIECE):
                 multiply(slot, o)
-        for slot in range(HEAD, N, GROUP):
+        for slot in range(HEAD, N, PIECE):
             for o in range(PASSES):
                 multiply(slot, o)
 
         def piece_peak(i):
-            own = neg_peak[:, PAGES + i : PAGES + i + 1]
+            own = neg_peak[:, i : i + 1]
             nc.vector.tensor_reduce(own, neg_peak[:, pages(i)], AX.X, ALU.min)
             weigh(i, own)
 
         for i in range(PIECES):
-            page_peaks(i)
-            if i > 0:
+            if i < PIECES - LATE:
+                page_peaks(i)
+            else:
+                nc.vector.tensor_reduce(neg_peak[:, i : i + 1], scores[i][:], AX.X, ALU.max, negate=True)
+            if 0 < i <= PIECES - LATE:
                 piece_peak(i - 1)
+            if i >= PIECES - LATE:
+                weigh(i, neg_peak[:, i : i + 1])
 
-        neg_max = neg_peak[:, PAGES + LAST :]
-        nc.vector.tensor_reduce(neg_max, neg_peak[:, pages(LAST - 1).start : PAGES + LAST - 1], AX.X, ALU.min)
-        nc.scalar.activation(peak[:], neg_peak[:], ACT.Exp, bias=neg_max, scale=-1.0)
-        weigh(LAST, neg_max)
-        nc.vector.scalar_tensor_tensor(scaled[:], sums[:], 1.0, peak[:, PAGES:], ALU.mult, ALU.mult, accum_out=total[:])
+        nc.vector.tensor_reduce(neg_max[:], neg_peak[:, 0:PIECES], AX.X, ALU.min)
+        nc.scalar.activation(peak[:, 0 : PIECES + EARLY_PAGES], neg_peak[:], ACT.Exp, bias=neg_max[:], scale=-1.0)
+        for n in range(LATE):
+            nc.vector.tensor_reduce(late_peak[:, n, :], weights[PIECES - LATE + n][:].rearrange("p (j s) -> p j s", s=SEG), AX.X, ALU.max)
+        nc.vector.scalar_tensor_tensor(scaled[:], sums[:], 1.0, peak[:, 0:PIECES], ALU.mult, ALU.mult, accum_out=total[:])
+        nc.vector.tensor_tensor(
+            peak[:, PIECES + EARLY_PAGES :].rearrange("p (n j) -> p n j", n=LATE),
+            late_peak[:],
+            peak[:, PIECES - LATE : PIECES].unsqueeze(2).to_broadcast([P, LATE, PIECE // SEG]),
+            ALU.mult,
+        )
         nc.vector.reciprocal(inverse[:], total[:])
-        nc.vector.tensor_scalar(result[:], peak[:, 0:PAGES], inverse[:], None, ALU.mult)
+        nc.vector.tensor_scalar(result[:], peak[:, PIECES:], inverse[:], None, ALU.mult)
         nc.sync.dma_start(out[0], result[:])

@@ -27,14 +27,16 @@ BLOCKS = 4
 STRIPE = 16
 LINE = 4
 GATHER = 512
-PIECE = 128
-PIECES = N // PIECE
-LAST = PIECES - 1
+WIDTHS = (128,) * 8
+PIECES = len(WIDTHS)
+STARTS = tuple(sum(WIDTHS[:i]) for i in range(PIECES))
 HEAD = 512
 RUN = 256
 PAGES = N // SEG
-LATE = 3
-EARLY_PAGES = (PIECES - LATE) * PIECE // SEG
+HALF = PAGES // 2
+ROW = HALF + PIECES
+PAGED = (2, 3, 4)
+ORDER = (2, 0, 3, 1, 4, 5, 6, 7)
 
 
 def tile_attend_page_peak_kernel(tc, qT, k_words, k_scales, offs, out):
@@ -74,7 +76,7 @@ def tile_attend_page_peak_kernel(tc, qT, k_words, k_scales, offs, out):
         q_codes = [sb.tile([P, NQ], U32, name=f"q_codes{o}", align_bytes=64) for o in range(PASSES)]
         q_planes = [sb.tile([P, NQ], U8, name=f"q_planes{o}", align_bytes=64) for o in range(PASSES)]
         listed = [sb.tile([P, GATHER], U32, name=f"listed{c}", align_bytes=64) for c in range(N // GATHER)]
-        scores = [ps.tile([P, PIECE], F32, name=f"scores{i}") for i in range(PIECES)]
+        scores = [ps.tile([P, width], F32, name=f"scores{i}") for i, width in enumerate(WIDTHS)]
 
         for c in range(N // GATHER):
             nc.vector.tensor_copy(listed[c][:], word_pool[:].indirect(offsets[:, c * cols : (c + 1) * cols]))
@@ -85,107 +87,118 @@ def tile_attend_page_peak_kernel(tc, qT, k_words, k_scales, offs, out):
             )
 
         stages = (
-            (((0,), 0),),
-            (((0,), RUN), ((1,), 0)),
-            (((1,), RUN),) + tuple(((0, 1), slot) for slot in range(HEAD, N, RUN)),
+            (((0,), (0, 2)),),
+            (((0,), (1, 3)), ((1,), (0, 2))),
+            (((1,), (1, 3)), ((0, 1), (4, 5)), ((0, 1), (6, 7))),
         )
         k_codes = []
         place = {}
         for stage, runs in enumerate(stages):
-            width = RUN * sum(len(passes) for passes, first in runs)
+            width = RUN * sum(len(passes) for passes, pair in runs)
             tag = f"after_cast{stage - 1}" if stage else "k_first"
             k_codes.append(sb.tile([P, width], U16, name=f"k_codes{stage}", tag=tag, align_bytes=64))
             column = 0
-            for passes, first in runs:
+            for passes, pair in runs:
                 for o in passes:
-                    for slot in range(first, first + RUN, PIECE):
-                        place[slot, o] = (stage, column)
-                        column += PIECE
+                    for i in pair:
+                        place[i, o] = (stage, column)
+                        column += WIDTHS[i]
 
-        def separate(passes, first):
-            stage, column = place[first, passes[0]]
-            target = k_codes[stage][:, column : column + len(passes) * RUN]
-            c, lo = divmod(first, GATHER)
-            both = listed[c][:, lo : lo + RUN].bitcast(U16).rearrange("p (n o) -> p o n", o=PASSES)
-            if len(passes) == PASSES:
-                nc.vector.tensor_copy(target.rearrange("p (o n) -> p o n", o=PASSES), both)
-            else:
-                nc.vector.tensor_copy(target, both[:, passes[0], :])
+        def separate(passes, pair):
+            stage, column = place[pair[0], passes[0]]
+            target = k_codes[stage][:, column : column + len(passes) * RUN].rearrange("p (o i n) -> p o i n", o=len(passes), i=len(pair))
+            c, lo = divmod(pair[0], GATHER // WIDTHS[0])
+            both = listed[c][:].bitcast(U16).rearrange("p (i n o) -> p o i n", o=PASSES, n=WIDTHS[0])
+            step = pair[1] - pair[0]
+            nc.vector.tensor_copy(target, both[:, passes[0] : passes[-1] + 1, lo : lo + step + 1 : step, :])
 
         def quantise(o):
             nc.vector.quantize_mx(out=q_codes[o][:].bitcast(FP8X4), scales=q_planes[o][:], in_=q_bf[o][:].rearrange("p q t -> p (q t)"))
 
-        def multiply(slot, o):
-            stage, column = place[slot, o]
-            c, lo = divmod(slot, GATHER)
+        def multiply(i, o):
+            stage, column = place[i, o]
+            c, lo = divmod(STARTS[i], GATHER)
             nc.tensor.matmul_mx(
-                out=scores[slot // PIECE][:],
+                out=scores[i][:],
                 lhsT=q_codes[o][:].bitcast(FP8X4),
                 lhsT_scale=q_planes[o][:],
-                rhs=k_codes[stage][:, column : column + PIECE].bitcast(FP4X4),
-                rhs_scale=k_planes[c][:, o, lo : lo + PIECE],
+                rhs=k_codes[stage][:, column : column + WIDTHS[i]].bitcast(FP4X4),
+                rhs_scale=k_planes[c][:, o, lo : lo + WIDTHS[i]],
                 start=(o == 0),
                 stop=(o == PASSES - 1),
             )
 
-        neg_peak = sb.tile([P, PIECES + EARLY_PAGES], F32, name="neg_peak")
+        neg_peak = sb.tile([P, 2 * ROW], F32, name="neg_peak")
         neg_max = sb.tile([P, 1], F32, name="neg_max")
-        late_peak = sb.tile([P, LATE, PIECE // SEG], F32, name="late_peak")
+        plain_peak = sb.tile([P, PAGES], F32, name="plain_peak", tag="after_cast1", align_bytes=64)
         sums = sb.tile([P, PIECES], F32, name="sums")
-        weights = [sb.tile([P, PIECE], F32, name=f"weights{i}") for i in range(PIECES)]
-        peak = sb.tile([P, PIECES + PAGES], F32, name="peak")
+        weights = [sb.tile([P, width], F32, name=f"weights{i}") for i, width in enumerate(WIDTHS)]
+        peak = sb.tile([P, 2 * ROW], F32, name="peak")
         scaled = sb.tile([P, PIECES], F32, name="scaled")
         total = sb.tile([P, 1], F32, name="total")
         inverse = sb.tile([P, 1], F32, name="inverse")
         result = sb.tile([P, PAGES], F32, name="result")
 
         def pages(i):
-            return slice(PIECES + i * PIECE // SEG, PIECES + (i + 1) * PIECE // SEG)
+            return slice(STARTS[i] // SEG, (STARTS[i] + WIDTHS[i]) // SEG)
 
-        def page_peaks(i):
-            nc.vector.tensor_reduce(neg_peak[:, pages(i)], scores[i][:].rearrange("p (j s) -> p j s", s=SEG), AX.X, ALU.max, negate=True)
+        def columns(i):
+            skip = PIECES if pages(i).start >= HALF else 0
+            return slice(pages(i).start + skip, pages(i).stop + skip)
 
-        def weigh(i, shift):
-            nc.scalar.activation(weights[i][:], scores[i][:], ACT.Exp, bias=shift, accum_out=sums[:, i : i + 1])
+        def shift(i):
+            return neg_peak[:, HALF + i : HALF + i + 1]
+
+        def weigh(i):
+            nc.scalar.activation(weights[i][:], scores[i][:], ACT.Exp, bias=shift(i), accum_out=sums[:, i : i + 1])
 
         for stage, runs in enumerate(stages):
             for passes, first in runs:
                 separate(passes, first)
             if stage < PASSES:
                 quantise(stage)
+        head = HEAD // WIDTHS[0]
         for o in range(PASSES):
-            for slot in range(0, HEAD, PIECE):
-                multiply(slot, o)
-        for slot in range(HEAD, N, PIECE):
+            for i in ORDER[:head]:
+                multiply(i, o)
+        for i in ORDER[head:]:
             for o in range(PASSES):
-                multiply(slot, o)
+                multiply(i, o)
 
-        def piece_peak(i):
-            own = neg_peak[:, i : i + 1]
-            nc.vector.tensor_reduce(own, neg_peak[:, pages(i)], AX.X, ALU.min)
-            weigh(i, own)
-
-        for i in range(PIECES):
-            if i < PIECES - LATE:
-                page_peaks(i)
+        due = {}
+        for at, i in enumerate(ORDER):
+            if i in PAGED:
+                due[min(at + 2, PIECES - 3)] = i
+                nc.vector.tensor_reduce(neg_peak[:, columns(i)], scores[i][:].rearrange("p (j s) -> p j s", s=SEG), AX.X, ALU.max, negate=True)
             else:
-                nc.vector.tensor_reduce(neg_peak[:, i : i + 1], scores[i][:], AX.X, ALU.max, negate=True)
-            if 0 < i <= PIECES - LATE:
-                piece_peak(i - 1)
-            if i >= PIECES - LATE:
-                weigh(i, neg_peak[:, i : i + 1])
+                nc.vector.tensor_reduce(shift(i), scores[i][:], AX.X, ALU.max, negate=True)
+                weigh(i)
+            if at in due:
+                nc.vector.tensor_reduce(shift(due[at]), neg_peak[:, columns(due[at])], AX.X, ALU.min)
+                weigh(due[at])
 
-        nc.vector.tensor_reduce(neg_max[:], neg_peak[:, 0:PIECES], AX.X, ALU.min)
-        nc.scalar.activation(peak[:, 0 : PIECES + EARLY_PAGES], neg_peak[:], ACT.Exp, bias=neg_max[:], scale=-1.0)
-        for n in range(LATE):
-            nc.vector.tensor_reduce(late_peak[:, n, :], weights[PIECES - LATE + n][:].rearrange("p (j s) -> p j s", s=SEG), AX.X, ALU.max)
-        nc.vector.scalar_tensor_tensor(scaled[:], sums[:], 1.0, peak[:, 0:PIECES], ALU.mult, ALU.mult, accum_out=total[:])
-        nc.vector.tensor_tensor(
-            peak[:, PIECES + EARLY_PAGES :].rearrange("p (n j) -> p n j", n=LATE),
-            late_peak[:],
-            peak[:, PIECES - LATE : PIECES].unsqueeze(2).to_broadcast([P, LATE, PIECE // SEG]),
-            ALU.mult,
-        )
+        def from_weights(i):
+            nc.vector.tensor_reduce(plain_peak[:, pages(i)], weights[i][:].rearrange("p (j s) -> p j s", s=SEG), AX.X, ALU.max)
+
+        def rescale(lo, hi):
+            nc.vector.tensor_tensor(
+                peak[:, columns(lo).start : columns(hi - 1).stop].rearrange("p (n j) -> p n j", n=hi - lo),
+                plain_peak[:, pages(lo).start : pages(hi - 1).stop].rearrange("p (n j) -> p n j", n=hi - lo),
+                peak[:, HALF + lo : HALF + hi].unsqueeze(2).to_broadcast([P, hi - lo, WIDTHS[lo] // SEG]),
+                ALU.mult,
+            )
+
+        both = slice(min(columns(PAGED[0]).start, HALF), max(columns(PAGED[-1]).stop, ROW))
+        nc.vector.tensor_reduce(neg_max[:], neg_peak[:, HALF:ROW], AX.X, ALU.min)
+        nc.scalar.activation(peak[:, both], neg_peak[:, both], ACT.Exp, bias=neg_max[:], scale=-1.0)
+        for i in range(PIECES):
+            if i not in PAGED:
+                from_weights(i)
+        nc.vector.scalar_tensor_tensor(scaled[:], sums[:], 1.0, peak[:, HALF:ROW], ALU.mult, ALU.mult, accum_out=total[:])
+        rescale(0, PAGED[0])
+        rescale(PAGED[-1] + 1, PIECES)
         nc.vector.reciprocal(inverse[:], total[:])
-        nc.vector.tensor_scalar(result[:], peak[:, PIECES:], inverse[:], None, ALU.mult)
+        nc.vector.tensor_scalar(
+            result[:].rearrange("p (h j) -> p h j", h=2), peak[:].rearrange("p (h j) -> p h j", h=2)[:, :, 0:HALF], inverse[:], None, ALU.mult
+        )
         nc.sync.dma_start(out[0], result[:])

@@ -49,6 +49,7 @@ def tile_attend_page_peak_kernel(tc, qT, k_words, k_scales, offs, out):
         word_pool = sb.tile([P, T], U32, name="word_pool", align_bytes=64)
         byte_pool = sb.tile([P, T], U8, name="byte_pool", align_bytes=64)
         byte_listed = [sb.tile([P, GATHER], U8, name=f"byte_listed{c}", align_bytes=64) for c in range(N // GATHER)]
+        byte_again = sb.tile([P, GATHER], U8, name="byte_again", align_bytes=64)
         k_planes = [sb.tile([P, PASSES, GATHER], U8, name=f"k_planes{c}", align_bytes=64) for c in range(N // GATHER)]
 
         nc.vector.memset(byte_pool[0:ROW0, :].bitcast(I32), 0)
@@ -66,10 +67,13 @@ def tile_attend_page_peak_kernel(tc, qT, k_words, k_scales, offs, out):
         rows = BLOCKS * PASSES
         for c in range(N // GATHER):
             nc.vector.tensor_copy(byte_listed[c][:], byte_pool[:].indirect(offsets[:, c * cols : (c + 1) * cols]))
+            if c == 0:
+                nc.vector.tensor_copy(byte_again[:], byte_pool[:].indirect(offsets[:, 0:cols]))
             for quad in (0, 2, 1, 3):
+                source = byte_again if c == 0 and quad % 2 else byte_listed[c]
                 nc.sync.dma_start(
                     k_planes[c][QUADRANT * quad : QUADRANT * quad + BLOCKS, :, :].rearrange("p o n -> p (o n)").bitcast(I32),
-                    byte_listed[c][ROW0 + rows * quad : ROW0 + rows * (quad + 1), :].bitcast(I32),
+                    source[ROW0 + rows * quad : ROW0 + rows * (quad + 1), :].bitcast(I32),
                 )
 
         q_bf = [sb.tile([P, NQ, PACK], BF16, name=f"q_bf{o}", align_bytes=64) for o in range(PASSES)]

from contextlib import ExitStack

import concourse.mybir as mybir

T, D, NQ, N, SEG = 4096, 1024, 128, 1024, 32
FLOPS = 2 * NQ * D * N

F32 = mybir.dt.float32
BF16 = mybir.dt.bfloat16
I32 = mybir.dt.int32
U32 = mybir.dt.uint32
U16 = mybir.dt.uint16
U8 = mybir.dt.uint8
FP8X4 = mybir.dt.float8_e4m3fn_x4
FP4X4 = mybir.dt.float4_e2m1fn_x4
ACT = mybir.ActivationFunctionType
ALU = mybir.AluOpType
AX = mybir.AxisListType

P = 128
QUADRANT = 32
ROW0 = P - QUADRANT
PACK = 4
K_PASS = P * PACK
PASSES = D // K_PASS
BLOCKS = 4
STRIPE = 16
LINE = 4
GATHER = 512
WIDTHS = (128,) * 8
PIECES = len(WIDTHS)
STARTS = tuple(sum(WIDTHS[:i]) for i in range(PIECES))
HEAD = 512
RUN = 256
PAGES = N // SEG
HALF = PAGES // 2
ROW = HALF + PIECES
PAGED = (2, 3, 4)
ORDER = (2, 0, 3, 1, 4, 5, 6, 7)


def tile_attend_page_peak_kernel(tc, qT, k_words, k_scales, offs, out):
    nc = tc.nc
    with ExitStack() as ctx:
        sb = ctx.enter_context(tc.tile_pool(name="sb", bufs=1))
        ps = ctx.enter_context(tc.psum_pool(name="ps", bufs=1))

        offsets = sb.tile([P, N // STRIPE], U16, name="offsets")
        word_pool = sb.tile([P, T], U32, name="word_pool", align_bytes=64)
        byte_pool = sb.tile([P, T], U8, name="byte_pool", align_bytes=64)
        byte_listed = [sb.tile([P, GATHER], U8, name=f"byte_listed{c}", align_bytes=64) for c in range(N // GATHER)]
        byte_again = sb.tile([P, GATHER], U8, name="byte_again", align_bytes=64)
        k_planes = [sb.tile([P, PASSES, GATHER], U8, name=f"k_planes{c}", align_bytes=64) for c in range(N // GATHER)]

        nc.vector.memset(byte_pool[0:ROW0, :].bitcast(I32), 0)
        for c in range(N // GATHER):
            nc.vector.memset(k_planes[c][:].rearrange("p o n -> p (o n)").bitcast(I32), 0)

        nc.sync.dma_start(byte_pool[ROW0:P, :].bitcast(I32), k_scales.rearrange("o f token -> f o token").bitcast(I32))
        nc.sync.dma_start(offsets[:], offs)
        nc.sync.dma_start(word_pool[:].bitcast(I32), k_words[0].rearrange("p token b -> p (token b)").bitcast(I32))
        q_raw = [sb.tile([P, PACK, NQ], F32, name=f"q_raw{o}", tag=f"after_cast{o}", align_bytes=64) for o in range(PASSES)]
        for o in range(PASSES):
            nc.sync.dma_start(q_raw[o][:], qT[0, o * K_PASS : (o + 1) * K_PASS, :].rearrange("(p t) q -> p t q", t=PACK))

        cols = GATHER // STRIPE
        rows = BLOCKS * PASSES
        for c in range(N // GATHER):
            nc.vector.tensor_copy(byte_listed[c][:], byte_pool[:].indirect(offsets[:, c * cols : (c + 1) * cols]))
            if c == 0:
                nc.vector.tensor_copy(byte_again[:], byte_pool[:].indirect(offsets[:, 0:cols]))
            for quad in (0, 2, 1, 3):
                source = byte_again if c == 0 and quad % 2 else byte_listed[c]
                nc.sync.dma_start(
                    k_planes[c][QUADRANT * quad : QUADRANT * quad + BLOCKS, :, :].rearrange("p o n -> p (o n)").bitcast(I32),
                    source[ROW0 + rows * quad : ROW0 + rows * (quad + 1), :].bitcast(I32),
                )

        q_bf = [sb.tile([P, NQ, PACK], BF16, name=f"q_bf{o}", align_bytes=64) for o in range(PASSES)]
        q_codes = [sb.tile([P, NQ], U32, name=f"q_codes{o}", align_bytes=64) for o in range(PASSES)]
        q_planes = [sb.tile([P, NQ], U8, name=f"q_planes{o}", align_bytes=64) for o in range(PASSES)]
        listed = [sb.tile([P, GATHER], U32, name=f"listed{c}", align_bytes=64) for c in range(N // GATHER)]
        scores = [ps.tile([P, width], F32, name=f"scores{i}") for i, width in enumerate(WIDTHS)]

        for c in range(N // GATHER):
            nc.vector.tensor_copy(listed[c][:], word_pool[:].indirect(offsets[:, c * cols : (c + 1) * cols]))

        for o in range(PASSES):
            nc.scalar.activation(
                q_bf[o][:].rearrange("p (r i) t -> p r t i", i=LINE), q_raw[o][:].rearrange("p t (r i) -> p r t i", i=LINE), ACT.Copy
            )

        stages = (
            (((0,), (0, 2)),),
            (((0,), (1, 3)), ((1,), (0, 2))),
            (((1,), (1, 3)), ((0, 1), (4, 5)), ((0, 1), (6, 7))),
        )
        k_codes = []
        place = {}
        for stage, runs in enumerate(stages):
            width = RUN * sum(len(passes) for passes, pair in runs)
            tag = f"after_cast{stage - 1}" if stage else "k_first"
            k_codes.append(sb.tile([P, width], U16, name=f"k_codes{stage}", tag=tag, align_bytes=64))
            column = 0
            for passes, pair in runs:
                for o in passes:
                    for i in pair:
                        place[i, o] = (stage, column)
                        column += WIDTHS[i]

        def separate(passes, pair):
            stage, column = place[pair[0], passes[0]]
            target = k_codes[stage][:, column : column + len(passes) * RUN].rearrange("p (o i n) -> p o i n", o=len(passes), i=len(pair))
            c, lo = divmod(pair[0], GATHER // WIDTHS[0])
            both = listed[c][:].bitcast(U16).rearrange("p (i n o) -> p o i n", o=PASSES, n=WIDTHS[0])
            step = pair[1] - pair[0]
            nc.vector.tensor_copy(target, both[:, passes[0] : passes[-1] + 1, lo : lo + step + 1 : step, :])

        def quantise(o):
            nc.vector.quantize_mx(out=q_codes[o][:].bitcast(FP8X4), scales=q_planes[o][:], in_=q_bf[o][:].rearrange("p q t -> p (q t)"))

        def multiply(i, o):
            stage, column = place[i, o]
            c, lo = divmod(STARTS[i], GATHER)
            nc.tensor.matmul_mx(
                out=scores[i][:],
                lhsT=q_codes[o][:].bitcast(FP8X4),
                lhsT_scale=q_planes[o][:],
                rhs=k_codes[stage][:, column : column + WIDTHS[i]].bitcast(FP4X4),
                rhs_scale=k_planes[c][:, o, lo : lo + WIDTHS[i]],
                start=(o == 0),
                stop=(o == PASSES - 1),
            )

        neg_peak = sb.tile([P, 2 * ROW], F32, name="neg_peak")
        neg_max = sb.tile([P, 1], F32, name="neg_max")
        plain_peak = sb.tile([P, PAGES], F32, name="plain_peak", tag="after_cast1", align_bytes=64)
        sums = sb.tile([P, PIECES], F32, name="sums")
        weights = [sb.tile([P, width], F32, name=f"weights{i}") for i, width in enumerate(WIDTHS)]
        peak = sb.tile([P, 2 * ROW], F32, name="peak")
        scaled = sb.tile([P, PIECES], F32, name="scaled")
        total = sb.tile([P, 1], F32, name="total")
        inverse = sb.tile([P, 1], F32, name="inverse")
        result = sb.tile([P, PAGES], F32, name="result")

        def pages(i):
            return slice(STARTS[i] // SEG, (STARTS[i] + WIDTHS[i]) // SEG)

        def columns(i):
            skip = PIECES if pages(i).start >= HALF else 0
            return slice(pages(i).start + skip, pages(i).stop + skip)

        def shift(i):
            return neg_peak[:, HALF + i : HALF + i + 1]

        def weigh(i):
            nc.scalar.activation(weights[i][:], scores[i][:], ACT.Exp, bias=shift(i), accum_out=sums[:, i : i + 1])

        for stage, runs in enumerate(stages):
            for passes, first in runs:
                separate(passes, first)
            if stage < PASSES:
                quantise(stage)
        head = HEAD // WIDTHS[0]
        for o in range(PASSES):
            for i in ORDER[:head]:
                multiply(i, o)
        for i in ORDER[head:]:
            for o in range(PASSES):
                multiply(i, o)

        due = {}
        for at, i in enumerate(ORDER):
            if i in PAGED:
                due[min(at + 2, PIECES - 3)] = i
                nc.vector.tensor_reduce(neg_peak[:, columns(i)], scores[i][:].rearrange("p (j s) -> p j s", s=SEG), AX.X, ALU.max, negate=True)
            else:
                nc.vector.tensor_reduce(shift(i), scores[i][:], AX.X, ALU.max, negate=True)
                weigh(i)
            if at in due:
                nc.vector.tensor_reduce(shift(due[at]), neg_peak[:, columns(due[at])], AX.X, ALU.min)
                weigh(due[at])

        def from_weights(i):
            nc.vector.tensor_reduce(plain_peak[:, pages(i)], weights[i][:].rearrange("p (j s) -> p j s", s=SEG), AX.X, ALU.max)

        def rescale(lo, hi):
            nc.vector.tensor_tensor(
                peak[:, columns(lo).start : columns(hi - 1).stop].rearrange("p (n j) -> p n j", n=hi - lo),
                plain_peak[:, pages(lo).start : pages(hi - 1).stop].rearrange("p (n j) -> p n j", n=hi - lo),
                peak[:, HALF + lo : HALF + hi].unsqueeze(2).to_broadcast([P, hi - lo, WIDTHS[lo] // SEG]),
                ALU.mult,
            )

        both = slice(min(columns(PAGED[0]).start, HALF), max(columns(PAGED[-1]).stop, ROW))
        nc.vector.tensor_reduce(neg_max[:], neg_peak[:, HALF:ROW], AX.X, ALU.min)
        nc.scalar.activation(peak[:, both], neg_peak[:, both], ACT.Exp, bias=neg_max[:], scale=-1.0)
        for i in range(PIECES):
            if i not in PAGED:
                from_weights(i)
        nc.vector.scalar_tensor_tensor(scaled[:], sums[:], 1.0, peak[:, HALF:ROW], ALU.mult, ALU.mult, accum_out=total[:])
        rescale(0, PAGED[0])
        rescale(PAGED[-1] + 1, PIECES)
        nc.vector.reciprocal(inverse[:], total[:])
        nc.vector.tensor_scalar(
            result[:].rearrange("p (h j) -> p h j", h=2), peak[:].rearrange("p (h j) -> p h j", h=2)[:, :, 0:HALF], inverse[:], None, ALU.mult
        )
        nc.sync.dma_start(out[0], result[:])
